import numpy as np
import ml_dtypes


def mxq(x, axis, fmt="e4m3"):
    dtype, down = {"e4m3": (ml_dtypes.float8_e4m3fn, 7), "e5m2": (ml_dtypes.float8_e5m2, 14)}[fmt]
    v = np.moveaxis(np.asarray(x, np.float32).astype(ml_dtypes.bfloat16).astype(np.float64), axis, -1)
    blocks = v.reshape(v.shape[:-1] + (-1, 32))
    amax = np.abs(blocks).max(-1, keepdims=True)
    byte = np.maximum(np.where(amax > 0, np.frexp(amax)[1] - 1 + 127, 0) - down, 1)
    scale = np.exp2(byte - 127.0)
    codes = (blocks / scale).astype(np.float32).astype(dtype).astype(np.float64)
    return np.moveaxis((codes * scale).reshape(v.shape), -1, axis)


WIDE = False


def mx_kscale(k):
    if not WIDE:
        return np.ones(k)
    levels = np.array([10, -10, 5, -5, 0])
    if k % 512:
        return np.exp2(np.random.permutation(np.resize(levels, k // 32))).repeat(32)
    a = np.empty((k // 512, 16))
    for p in range(k // 512):
        a[p, :8] = np.random.permutation(np.resize(levels, 8))
        for g in range(8):
            far = levels[np.abs(levels - a[p, g]) >= 10]
            a[p, g + 8] = far[np.random.randint(len(far))]
    return np.exp2(a.ravel()).repeat(32)


def f64(x):
    return np.asarray(x).astype(np.float64)


def striped(idx):
    return np.tile(idx.reshape(-1, 16).T, (8, 1)).astype(np.uint16)


def unstriped(offs):
    return offs[:16].T.reshape(-1).astype(np.int64)


def striped8(idx):
    return np.concatenate([x.reshape(-1, 16).T for x in idx]).astype(np.uint16)


def runs(offs, k):
    lists = np.stack([offs[16 * r : 16 * r + 16].T.reshape(-1) for r in range(8)]).astype(np.int64)
    return lists[np.arange(k) % 512 // 64]


def pack_weight(w):
    k, n = w.shape
    w = f64(np.asarray(w, np.float32).astype(ml_dtypes.bfloat16)).reshape(k // 32, 32, n)
    amax = np.abs(w).max(1)
    byte = np.clip(np.where(amax > 0, np.frexp(amax)[1] - 1 + 127 - 7, 1), 1, 254)
    scaled = (w * np.exp2(127.0 - byte)[:, None, :]).reshape(k, n).astype(np.float32)
    words = np.ascontiguousarray(scaled.reshape(k // 512, 128, 4, n).transpose(0, 1, 3, 2)).astype(ml_dtypes.float8_e4m3fn).view(np.uint8)
    return words, np.ascontiguousarray(byte.astype(np.uint8).reshape(k // 512, 16, n))


def unpack_weight(words, scales):
    g, p, n, _ = words.shape
    vals = np.ascontiguousarray(words).view(ml_dtypes.float8_e4m3fn).astype(np.float64) * np.repeat(np.exp2(scales.astype(np.float64) - 127.0), 8, axis=1)[..., None]
    return vals.transpose(0, 1, 3, 2).reshape(g * 512, n)


K, T, S, H, C = 512, 2048, 512, 512, 512


def setup_inputs():
    n = np.random.standard_normal
    s = mx_kscale(K)[:, None]
    packed_xT = pack_weight(n((K, T)) * s)
    return {
        "x_words": packed_xT[0],
        "x_scales": packed_xT[1],
        "w1": (n((K, H)) / np.sqrt(K) / s).astype(np.float32),
        "gs": (np.random.uniform(0.5, 1.5, (K, 1)) / s).astype(np.float32),
        "offs": striped(np.random.permutation(T)[:S]),
        "n1": striped(np.random.permutation(S)),
        "n2": striped(np.random.permutation(S)),
        "ca": striped(np.random.permutation(T)[:C]),
        "hc": striped8(np.random.randint(0, T, (8, C))),
        "n3": striped(np.random.permutation(S)),
        "n4": striped(np.random.permutation(S)),
    }


def reference(x_words, x_scales, w1, gs, offs, n1, n2, ca, hc, n3, n4):
    x_ca = unpack_weight(x_words, x_scales)[:, unstriped(ca)]
    xq = unpack_weight(x_words, x_scales)[:, unstriped(offs)]
    y = mxq(f64(w1), 0, "e4m3").T @ xq
    st = y - y[:, unstriped(n1)]
    z = f64(gs) * (np.maximum(st, st[:, unstriped(n2)]))
    zq = mxq(z, 0, "e4m3")
    a = 0.0625 * (x_ca.T @ zq)
    x_hc = unpack_weight(x_words, x_scales)[np.arange(K)[:, None], runs(hc, K)]
    b = 0.0625 * (x_hc.T @ zq)
    return (a - a[:, unstriped(n3)]) / (np.abs(b) + np.abs(b[:, unstriped(n4)]) + 0.5)

@@ -1,0 +1,297 @@
+from contextlib import ExitStack
+
+import concourse.mybir as mybir
+from concourse.masks import make_identity
+
+K, T, S, H, C = 512, 2048, 512, 512, 512
+FLOPS = 2 * K * H * S + 2 * 2 * K * C * S
+
+F32 = mybir.dt.float32
+BF16 = mybir.dt.bfloat16
+I32 = mybir.dt.int32
+U32 = mybir.dt.uint32
+U16 = mybir.dt.uint16
+U8 = mybir.dt.uint8
+FP8X4 = mybir.dt.float8_e4m3fn_x4
+ALU = mybir.AluOpType
+ACT = mybir.ActivationFunctionType
+
+P = 128
+PACK = 4
+HALF = S // 2
+LIST_COLS = S // 16
+
+
+def tile_picked_cdhnormbhopmx_none_p_kernel(tc, x_words, x_scales, w1, gs, offs, n1, n2, ca, hc, n3, n4, out):
+    nc = tc.nc
+    with ExitStack() as ctx:
+        keep = ctx.enter_context(tc.tile_pool(name="keep", bufs=1))
+        psum = ctx.enter_context(tc.psum_pool(name="psum", bufs=1))
+
+        def load_list(src, name):
+            tile = keep.tile([P, LIST_COLS], U16, name=name)
+            nc.sync.dma_start(tile[:], src)
+            return tile
+
+        def half_cols(h):
+            return slice(h * HALF, (h + 1) * HALF)
+
+        def gather_half(engine, dst, window, offsets, h):
+            picked = window.indirect(offsets[:, h * LIST_COLS // 2 : (h + 1) * LIST_COLS // 2])
+            if engine == "v":
+                nc.vector.tensor_copy(dst, picked)
+            else:
+                nc.scalar.activation(dst, picked, ACT.Copy)
+
+        offs_sb = load_list(offs, "offs_sb")
+        ca_sb = load_list(ca, "ca_sb")
+        hc_sb = load_list(hc, "hc_sb")
+        xs = keep.tile([P, T], U8, name="xs")
+        for q in range(4):
+            nc.sync.dma_start(
+                xs[32 * q : 32 * q + 32, :].bitcast(I32),
+                x_scales[0, 4 * q : 4 * q + 4, :].bitcast(I32).partition_broadcast(8),
+            )
+        xw = keep.tile([P, T], I32, name="xw")
+        nc.sync.dma_start(xw[:], x_words[0].rearrange("p n r -> p (n r)").bitcast(I32))
+        w_rows = w1.rearrange("(p j) c -> p j c", j=PACK)
+        w_raw = []
+        for h in range(2):
+            raw = keep.tile([P, PACK, H // 2], F32, name="w_raw%d" % h)
+            nc.sync.dma_start(raw[:], w_rows[:, :, h * H // 2 : (h + 1) * H // 2])
+            w_raw.append(raw)
+        n1_sb = load_list(n1, "n1_sb")
+        n2_sb = load_list(n2, "n2_sb")
+        gs_sb = keep.tile([P, PACK], F32, name="gs_sb")
+        nc.sync.dma_start(gs_sb[:], gs.rearrange("(p t) o -> p (t o)", t=PACK))
+        n4_sb = load_list(n4, "n4_sb")
+        n3_sb = load_list(n3, "n3_sb")
+
+        gs_abs = keep.tile([P, PACK], F32, name="gs_abs")
+        nc.scalar.activation(gs_abs[:], gs_sb[:], ACT.Abs)
+        gs_sign = keep.tile([P, PACK], BF16, name="gs_sign")
+        nc.scalar.activation(gs_sign[:], gs_sb[:], ACT.Sign)
+        ident = keep.tile([P, P], F32, name="ident")
+        make_identity(nc, ident[:])
+        hc_scales = keep.tile([P, C], U8, name="hc_scales", align_bytes=64)
+        nc.gpsimd.memset(hc_scales[:], 0)
+
+        tok_scales = keep.tile([P, S], U8, name="tok_scales", align_bytes=64)
+        tok_words = keep.tile([P, S], U32, name="tok_words", align_bytes=64)
+        ca_scales = keep.tile([P, C], U8, name="ca_scales", align_bytes=64)
+        hc_picked = keep.tile([P, C], U8, name="hc_picked", align_bytes=64)
+        nc.vector.tensor_copy(tok_scales[:], xs[:].indirect(offs_sb[:]))
+        nc.vector.tensor_copy(tok_words[:], xw[:].bitcast(U32).indirect(offs_sb[:]))
+        nc.vector.tensor_copy(ca_scales[:], xs[:].indirect(ca_sb[:]))
+        nc.vector.tensor_copy(hc_picked[:], xs[:].indirect(hc_sb[:]))
+        for r in range(4):
+            first = r if r < 2 else 16 + r
+            nc.sync.dma_start(hc_scales[r:P:32, :].bitcast(I32), hc_picked[first:P:32, :].bitcast(I32))
+
+        w_bf = keep.tile([P, PACK, P, PACK], BF16, name="w_bf", tag="w_bf", align_bytes=64)
+
+        def cast_w(on_vector, m0, m1):
+            h = m0 // 64
+            src = w_raw[h][:, :, PACK * (m0 - 64 * h) : PACK * (m1 - 64 * h)].rearrange("p j (m t) -> p m t j", t=PACK)
+            dst = w_bf[:, :, m0:m1, :].rearrange("p t m j -> p m t j")
+            if on_vector:
+                nc.vector.tensor_copy(dst, src)
+            else:
+                nc.scalar.copy(dst, src)
+
+        cast_w(False, 0, 64)
+        cast_w(False, 64, 88)
+        cast_w(True, 88, 128)
+        w_codes = keep.tile([P, PACK, P], U32, name="w_codes", align_bytes=64)
+        w_scales = keep.tile([P, PACK, P], U8, name="w_scales", align_bytes=64)
+        y_ps = []
+        for t in range(PACK):
+            nc.vector.quantize_mx(
+                out=w_codes[:, t, :].bitcast(FP8X4),
+                scales=w_scales[:, t, :],
+                in_=w_bf[:, t, :, :].rearrange("p m j -> p (m j)"),
+            )
+            acc = psum.tile([P, S], F32, name="y_ps%d" % t, tag="bank%d" % t)
+            nc.tensor.matmul_mx(
+                out=acc[:],
+                lhsT=w_codes[:, t, :].bitcast(FP8X4),
+                lhsT_scale=w_scales[:, t, :],
+                rhs=tok_words[:].bitcast(FP8X4),
+                rhs_scale=tok_scales[:],
+                start=True,
+                stop=True,
+            )
+            y_ps.append(acc)
+
+        cand_words = keep.tile([P, 2, C], U32, name="cand_words", tag="w_bf", align_bytes=64)
+        y_sb = [keep.tile([P, S], F32, name="y_sb%d" % t) for t in range(PACK)]
+        y_at = [keep.tile([P, S], F32, name="y_at%d" % t) for t in range(PACK)]
+        st_all = keep.tile([P, PACK, S], F32, name="st_all")
+        st_at = [keep.tile([P, PACK, HALF], F32, name="st_at%d" % h) for h in range(2)]
+
+        def cand(which, lst):
+            nc.vector.tensor_copy(cand_words[:, which, :], xw[:].bitcast(U32).indirect(lst[:]))
+
+        def y_out(t):
+            nc.scalar.activation(y_sb[t][:], y_ps[t][:], ACT.Identity, scale=gs_abs[:, t : t + 1])
+
+        def hop1(t, engines):
+            for h in range(2):
+                gather_half(engines[h], y_at[t][:, half_cols(h)], y_sb[t][:], n1_sb, h)
+
+        def diff(t, engine="v"):
+            if engine == "g":
+                nc.gpsimd.tensor_tensor(st_all[:, t, :], y_sb[t][:], y_at[t][:], ALU.subtract)
+            else:
+                nc.vector.scalar_tensor_tensor(st_all[:, t, :], y_ps[t][:], gs_abs[:, t : t + 1], y_at[t][:], ALU.mult, ALU.subtract)
+
+        def hop2(t, h, engine):
+            gather_half(engine, st_at[h][:, t, :], st_all[:, t, :], n2_sb, h)
+
+        y_out(0)
+        y_out(1)
+        cand(1, hc_sb)
+        hop1(0, "sv")
+        hop1(1, "sv")
+        y_out(2)
+        diff(0)
+        y_out(3)
+        diff(1)
+        hop1(2, "ss")
+        cand(0, ca_sb)
+        hop1(3, "sv")
+        hop2(0, 0, "s")
+        diff(2)
+        hop2(1, 0, "s")
+        diff(3)
+        hop2(2, 0, "s")
+        hop2(3, 0, "v")
+        for t in range(PACK):
+            hop2(t, 1, "s")
+
+        b_abs = [keep.tile([P, S], F32, name="b_abs%d" % i) for i in range(4)]
+        a_sb = [keep.tile([P, S], F32, name="a_sb%d" % i) for i in range(4)]
+        sign_wide = gs_sign[:].unsqueeze(1).to_broadcast([P, HALF // 2, PACK])
+        scores = {}
+
+        def quantise_z(h):
+            z_abs = keep.tile([P, HALF, PACK], BF16, name="z_abs%d" % h, tag="z_%d" % (2 * h), align_bytes=64)
+            z_bf = keep.tile([P, HALF, PACK], BF16, name="z_bf%d" % h, tag="z_%d" % (2 - h), align_bytes=64)
+            z_codes = keep.tile([P, HALF], U32, name="z_codes%d" % h, align_bytes=64)
+            z_scales = keep.tile([P, HALF], U8, name="z_scales%d" % h, align_bytes=64)
+            quarters = [slice(u * HALF // 2, (u + 1) * HALF // 2) for u in range(2)]
+            for q in quarters:
+                nc.vector.tensor_tensor(
+                    z_abs[:, q, :].rearrange("p (c i) t -> p c t i", i=4),
+                    st_all[:, :, half_cols(h)][:, :, q].rearrange("p t (c i) -> p c t i", i=4),
+                    st_at[h][:, :, q].rearrange("p t (c i) -> p c t i", i=4),
+                    ALU.max,
+                )
+            for q in quarters:
+                nc.vector.tensor_tensor(z_bf[:, q, :], z_abs[:, q, :], sign_wide, ALU.mult)
+            for q in quarters:
+                nc.vector.quantize_mx(
+                    out=z_codes[:, q].bitcast(FP8X4), scales=z_scales[:, q], in_=z_bf[:, q, :].rearrange("p n t -> p (n t)")
+                )
+            for which, scales in ((1, hc_scales), (0, ca_scales)):
+                for pair in range(2):
+                    acc = psum.tile([P, 2, HALF], F32, name="sc%d%d%d" % (which, pair, h), tag="bank%d" % (4 * (1 - h) + 2 * which + pair))
+                    for e in range(2):
+                        rows = slice((2 * pair + e) * P, (2 * pair + e + 1) * P)
+                        nc.tensor.matmul_mx(
+                            out=acc[:, e, :],
+                            lhsT=cand_words[:, which, rows].bitcast(FP8X4),
+                            lhsT_scale=scales[:, rows],
+                            rhs=z_codes[:].bitcast(FP8X4),
+                            rhs_scale=z_scales[:],
+                            start=True,
+                            stop=True,
+                        )
+                        scores[which, 2 * pair + e, h] = acc[:, e, :]
+
+        def b_out(i, h):
+            nc.scalar.activation(b_abs[i][:, half_cols(h)], scores[1, i, h], ACT.Abs)
+
+        def a_out(i, h, engine):
+            if engine == "v":
+                nc.vector.tensor_copy(a_sb[i][:, half_cols(h)], scores[0, i, h])
+            else:
+                nc.scalar.copy(a_sb[i][:, half_cols(h)], scores[0, i, h])
+
+        b_at = [keep.tile([P, S], F32, name="b_at%d" % i) for i in range(4)]
+        a_at = [keep.tile([P, S], F32, name="a_at%d" % i) for i in range(4)]
+        num = [keep.tile([P, S], F32, name="num%d" % i) for i in range(4)]
+        den_t = {}
+        root_t = {}
+        inv = {}
+
+        def hop_b(i, engines):
+            for h in range(2):
+                gather_half(engines[h], b_at[i][:, half_cols(h)], b_abs[i][:], n4_sb, h)
+            den_t[i] = psum.tile([P, 4, P], F32, name="den_t%d" % i, tag="bank%d" % (4 + i))
+            for c in range(4):
+                blk = slice(c * P, (c + 1) * P)
+                nc.tensor.matmul(den_t[i][:, c, :], b_at[i][:, blk], ident[:], start=True, stop=False, is_transpose=True)
+                nc.tensor.matmul(den_t[i][:, c, :], b_abs[i][:, blk], ident[:], start=False, stop=True, is_transpose=True)
+
+        def root(i):
+            root_t[i] = keep.tile([P, 4, P], F32, name="root_t%d" % i)
+            nc.scalar.activation(root_t[i][:], den_t[i][:], ACT.Abs_reciprocal_sqrt, bias=8.0)
+
+        def square(i, engine="s"):
+            inv_t = keep.tile([P, 4, P], F32, name="inv_t%d" % i)
+            if engine == "g":
+                nc.gpsimd.tensor_tensor(inv_t[:], root_t[i][:], root_t[i][:], ALU.mult)
+            else:
+                nc.scalar.activation(inv_t[:], root_t[i][:], ACT.Square)
+            inv[i] = psum.tile([P, S], F32, name="inv%d" % i, tag="bank%d" % i)
+            for c in range(4):
+                nc.tensor.transpose(inv[i][:, c * P : (c + 1) * P], inv_t[:, c, :], ident[:])
+
+        def hop_a(i, engines):
+            for h in range(2):
+                gather_half(engines[h], a_at[i][:, half_cols(h)], a_sb[i][:], n3_sb, h)
+
+        def numer(i, engine="v", cols=slice(0, S)):
+            (nc.gpsimd if engine == "g" else nc.vector).tensor_tensor(num[i][:, cols], a_sb[i][:, cols], a_at[i][:, cols], ALU.subtract)
+
+        def finish(i, cols=slice(0, S)):
+            res = keep.tile([P, cols.stop - cols.start], F32, name="res%d_%d" % (i, cols.start))
+            nc.vector.tensor_tensor(res[:], inv[i][:, cols], num[i][:, cols], ALU.mult)
+            nc.sync.dma_start(out[i * P : (i + 1) * P, cols], res[:])
+
+        quantise_z(0)
+        [b_out(i, 0) for i in range(4)]
+        [a_out(i, 0, "s") for i in range(4)]
+        quantise_z(1)
+        [b_out(i, 1) for i in range(4)]
+        a_out(0, 1, "v")
+        a_out(1, 1, "v")
+        hop_b(0, "vv")
+        hop_b(1, "ss")
+        hop_b(2, "vv")
+        hop_b(3, "ss")
+        a_out(2, 1, "v")
+        a_out(3, 1, "v")
+        root(0)
+        root(1)
+        hop_a(0, "vv")
+        square(0)
+        square(1)
+        numer(0)
+        root(2)
+        root(3)
+        hop_a(1, "vv")
+        finish(0)
+        numer(1)
+        square(2)
+        square(3)
+        finish(1)
+        hop_a(2, "sv")
+        numer(2)
+        hop_a(3, "ss")
+        finish(2)
+        numer(3, "v", half_cols(0))
+        numer(3, "v", half_cols(1))
+        finish(3, half_cols(0))
+        finish(3, half_cols(1))

@@ -1,7 +1,6 @@
 from contextlib import ExitStack
 
 import concourse.mybir as mybir
-from concourse.masks import make_identity
 
 K, T, S, H, C = 512, 2048, 512, 512, 512
 FLOPS = 2 * K * H * S + 2 * 2 * K * C * S
@@ -36,16 +35,22 @@ def tile_picked_cdhnormbhopmx_none_p_kernel(tc, x_words, x_scales, w1, gs, offs,
         def half_cols(h):
             return slice(h * HALF, (h + 1) * HALF)
 
-        def gather_half(engine, dst, window, offsets, h):
-            picked = window.indirect(offsets[:, h * LIST_COLS // 2 : (h + 1) * LIST_COLS // 2])
+        def gather(engine, dst, window, offsets, cols):
+            picked = window.indirect(offsets[:, cols.start // 16 : cols.stop // 16])
             if engine == "v":
                 nc.vector.tensor_copy(dst, picked)
             else:
                 nc.scalar.activation(dst, picked, ACT.Copy)
 
+        def gather_half(engine, dst, window, offsets, h):
+            gather(engine, dst, window, offsets, half_cols(h))
+
         offs_sb = load_list(offs, "offs_sb")
         ca_sb = load_list(ca, "ca_sb")
         hc_sb = load_list(hc, "hc_sb")
+        warm = keep.tile([P, 1], F32, name="warm")
+        nc.vector.memset(warm[:], 1.0)
+        nc.scalar.activation(warm[:], warm[:], ACT.Abs_reciprocal_sqrt)
         xs = keep.tile([P, T], U8, name="xs")
         for q in range(4):
             nc.sync.dma_start(
@@ -71,8 +76,6 @@ def tile_picked_cdhnormbhopmx_none_p_kernel(tc, x_words, x_scales, w1, gs, offs,
         nc.scalar.activation(gs_abs[:], gs_sb[:], ACT.Abs)
         gs_sign = keep.tile([P, PACK], BF16, name="gs_sign")
         nc.scalar.activation(gs_sign[:], gs_sb[:], ACT.Sign)
-        ident = keep.tile([P, P], F32, name="ident")
-        make_identity(nc, ident[:])
         hc_scales = keep.tile([P, C], U8, name="hc_scales", align_bytes=64)
         nc.gpsimd.memset(hc_scales[:], 0)
 
@@ -123,17 +126,21 @@ def tile_picked_cdhnormbhopmx_none_p_kernel(tc, x_words, x_scales, w1, gs, offs,
             )
             y_ps.append(acc)
 
-        cand_words = keep.tile([P, 2, C], U32, name="cand_words", tag="w_bf", align_bytes=64)
-        y_sb = [keep.tile([P, S], F32, name="y_sb%d" % t) for t in range(PACK)]
-        y_at = [keep.tile([P, S], F32, name="y_at%d" % t) for t in range(PACK)]
+        cand_words = {}
+        y_sb = [keep.tile([P, S], F32, name="y_sb%d" % t, tag="y_sb%d" % t, align_bytes=64) for t in range(PACK)]
+        y_at = [keep.tile([P, S], F32, name="y_at%d" % t, tag="y_at%d" % t, align_bytes=64) for t in range(PACK)]
         st_all = keep.tile([P, PACK, S], F32, name="st_all")
-        st_at = [keep.tile([P, PACK, HALF], F32, name="st_at%d" % h) for h in range(2)]
+        st_at = {}
 
-        def cand(which, lst):
-            nc.vector.tensor_copy(cand_words[:, which, :], xw[:].bitcast(U32).indirect(lst[:]))
+        def cand(which, lst, tag):
+            cand_words[which] = keep.tile([P, C], U32, name="cand_words%d" % which, tag=tag, align_bytes=64)
+            nc.vector.tensor_copy(cand_words[which][:], xw[:].bitcast(U32).indirect(lst[:]))
 
-        def y_out(t):
-            nc.scalar.activation(y_sb[t][:], y_ps[t][:], ACT.Identity, scale=gs_abs[:, t : t + 1])
+        def y_out(t, engine="s"):
+            if engine == "s":
+                nc.scalar.activation(y_sb[t][:], y_ps[t][:], ACT.Identity, scale=gs_abs[:, t : t + 1])
+            else:
+                nc.vector.tensor_scalar(y_sb[t][:], y_ps[t][:], gs_abs[:, t : t + 1], None, ALU.mult)
 
         def hop1(t, engines):
             for h in range(2):
@@ -145,153 +152,179 @@ def tile_picked_cdhnormbhopmx_none_p_kernel(tc, x_words, x_scales, w1, gs, offs,
             else:
                 nc.vector.scalar_tensor_tensor(st_all[:, t, :], y_ps[t][:], gs_abs[:, t : t + 1], y_at[t][:], ALU.mult, ALU.subtract)
 
-        def hop2(t, h, engine):
+        def hop2(t, h, engine, tag=None):
+            if h not in st_at:
+                st_at[h] = keep.tile([P, PACK, HALF], F32, name="st_at%d" % h, tag=tag or "st_at%d" % h, align_bytes=64)
             gather_half(engine, st_at[h][:, t, :], st_all[:, t, :], n2_sb, h)
-
-        y_out(0)
-        y_out(1)
-        cand(1, hc_sb)
-        hop1(0, "sv")
-        hop1(1, "sv")
-        y_out(2)
-        diff(0)
-        y_out(3)
-        diff(1)
-        hop1(2, "ss")
-        cand(0, ca_sb)
-        hop1(3, "sv")
-        hop2(0, 0, "s")
-        diff(2)
-        hop2(1, 0, "s")
-        diff(3)
-        hop2(2, 0, "s")
-        hop2(3, 0, "v")
-        for t in range(PACK):
-            hop2(t, 1, "s")
 
         b_abs = [keep.tile([P, S], F32, name="b_abs%d" % i) for i in range(4)]
         a_sb = [keep.tile([P, S], F32, name="a_sb%d" % i) for i in range(4)]
-        sign_wide = gs_sign[:].unsqueeze(1).to_broadcast([P, HALF // 2, PACK])
-        scores = {}
+        z_codes = keep.tile([P, S], U32, name="z_codes", align_bytes=64)
+        z_scales = keep.tile([P, S], U8, name="z_scales", align_bytes=64)
+        QW = S // 4
+        sign_wide = gs_sign[:].unsqueeze(1).to_broadcast([P, QW, PACK])
+        z_abs = {}
+        z_bf = {}
+        acc = {}
 
-        def quantise_z(h):
-            z_abs = keep.tile([P, HALF, PACK], BF16, name="z_abs%d" % h, tag="z_%d" % (2 * h), align_bytes=64)
-            z_bf = keep.tile([P, HALF, PACK], BF16, name="z_bf%d" % h, tag="z_%d" % (2 - h), align_bytes=64)
-            z_codes = keep.tile([P, HALF], U32, name="z_codes%d" % h, align_bytes=64)
-            z_scales = keep.tile([P, HALF], U8, name="z_scales%d" % h, align_bytes=64)
-            quarters = [slice(u * HALF // 2, (u + 1) * HALF // 2) for u in range(2)]
-            for q in quarters:
-                nc.vector.tensor_tensor(
-                    z_abs[:, q, :].rearrange("p (c i) t -> p c t i", i=4),
-                    st_all[:, :, half_cols(h)][:, :, q].rearrange("p t (c i) -> p c t i", i=4),
-                    st_at[h][:, :, q].rearrange("p t (c i) -> p c t i", i=4),
-                    ALU.max,
+        def z_max(q, tag=None):
+            z_abs[q] = keep.tile([P, QW, PACK], BF16, name="z_abs%d" % q, tag=tag or "z_abs%d" % q, align_bytes=64)
+            cols = slice(q * QW, (q + 1) * QW)
+            nc.vector.tensor_tensor(
+                z_abs[q][:].rearrange("p (c i) t -> p c t i", i=4),
+                st_all[:, :, cols].rearrange("p t (c i) -> p c t i", i=4),
+                st_at[q // 2][:, :, (q % 2) * QW : (q % 2 + 1) * QW].rearrange("p t (c i) -> p c t i", i=4),
+                ALU.max,
+            )
+
+        def z_sign(q):
+            z_bf[q] = keep.tile([P, QW, PACK], BF16, name="z_bf%d" % q, tag="z_bf%d" % q, align_bytes=64)
+            nc.vector.tensor_tensor(z_bf[q][:], z_abs[q][:], sign_wide, ALU.mult)
+
+        def z_quant(q):
+            cols = slice(q * QW, (q + 1) * QW)
+            nc.vector.quantize_mx(
+                out=z_codes[:, cols].bitcast(FP8X4), scales=z_scales[:, cols], in_=z_bf[q][:].rearrange("p n t -> p (n t)")
+            )
+
+        def score(which, c0, c1):
+            scales = hc_scales if which == 1 else ca_scales
+            for i in range(4):
+                if (which, i) not in acc:
+                    acc[which, i] = psum.tile([P, S], F32, name="sc%d%d" % (which, i), tag="bank%d" % (4 * which + i))
+                rows = slice(i * P, (i + 1) * P)
+                nc.tensor.matmul_mx(
+                    out=acc[which, i][:, c0:c1],
+                    lhsT=cand_words[which][:, rows].bitcast(FP8X4),
+                    lhsT_scale=scales[:, rows],
+                    rhs=z_codes[:, c0:c1].bitcast(FP8X4),
+                    rhs_scale=z_scales[:, c0:c1],
+                    start=True,
+                    stop=True,
                 )
-            for q in quarters:
-                nc.vector.tensor_tensor(z_bf[:, q, :], z_abs[:, q, :], sign_wide, ALU.mult)
-            for q in quarters:
-                nc.vector.quantize_mx(
-                    out=z_codes[:, q].bitcast(FP8X4), scales=z_scales[:, q], in_=z_bf[:, q, :].rearrange("p n t -> p (n t)")
-                )
-            for which, scales in ((1, hc_scales), (0, ca_scales)):
-                for pair in range(2):
-                    acc = psum.tile([P, 2, HALF], F32, name="sc%d%d%d" % (which, pair, h), tag="bank%d" % (4 * (1 - h) + 2 * which + pair))
-                    for e in range(2):
-                        rows = slice((2 * pair + e) * P, (2 * pair + e + 1) * P)
-                        nc.tensor.matmul_mx(
-                            out=acc[:, e, :],
-                            lhsT=cand_words[:, which, rows].bitcast(FP8X4),
-                            lhsT_scale=scales[:, rows],
-                            rhs=z_codes[:].bitcast(FP8X4),
-                            rhs_scale=z_scales[:],
-                            start=True,
-                            stop=True,
-                        )
-                        scores[which, 2 * pair + e, h] = acc[:, e, :]
 
-        def b_out(i, h):
-            nc.scalar.activation(b_abs[i][:, half_cols(h)], scores[1, i, h], ACT.Abs)
+        def b_out(i, c0, c1):
+            nc.scalar.activation(b_abs[i][:, c0:c1], acc[1, i][:, c0:c1], ACT.Abs)
 
-        def a_out(i, h, engine):
+        def a_out(i, engine, c0=0, c1=S):
             if engine == "v":
-                nc.vector.tensor_copy(a_sb[i][:, half_cols(h)], scores[0, i, h])
+                nc.vector.tensor_copy(a_sb[i][:, c0:c1], acc[0, i][:, c0:c1])
             else:
-                nc.scalar.copy(a_sb[i][:, half_cols(h)], scores[0, i, h])
+                nc.scalar.copy(a_sb[i][:, c0:c1], acc[0, i][:, c0:c1])
 
         b_at = [keep.tile([P, S], F32, name="b_at%d" % i) for i in range(4)]
         a_at = [keep.tile([P, S], F32, name="a_at%d" % i) for i in range(4)]
         num = [keep.tile([P, S], F32, name="num%d" % i) for i in range(4)]
-        den_t = {}
+        den = {}
         root_t = {}
         inv = {}
 
         def hop_b(i, engines):
             for h in range(2):
                 gather_half(engines[h], b_at[i][:, half_cols(h)], b_abs[i][:], n4_sb, h)
-            den_t[i] = psum.tile([P, 4, P], F32, name="den_t%d" % i, tag="bank%d" % (4 + i))
-            for c in range(4):
-                blk = slice(c * P, (c + 1) * P)
-                nc.tensor.matmul(den_t[i][:, c, :], b_at[i][:, blk], ident[:], start=True, stop=False, is_transpose=True)
-                nc.tensor.matmul(den_t[i][:, c, :], b_abs[i][:, blk], ident[:], start=False, stop=True, is_transpose=True)
+
+        def denom(i, engine):
+            den[i] = keep.tile([P, S], F32, name="den%d" % i)
+            (nc.gpsimd if engine == "g" else nc.vector).tensor_tensor(den[i][:], b_abs[i][:], b_at[i][:], ALU.add)
 
         def root(i):
-            root_t[i] = keep.tile([P, 4, P], F32, name="root_t%d" % i)
-            nc.scalar.activation(root_t[i][:], den_t[i][:], ACT.Abs_reciprocal_sqrt, bias=8.0)
+            root_t[i] = keep.tile([P, S], F32, name="root_t%d" % i)
+            nc.scalar.activation(root_t[i][:], den[i][:], ACT.Abs_reciprocal_sqrt, bias=8.0)
 
-        def square(i, engine="s"):
-            inv_t = keep.tile([P, 4, P], F32, name="inv_t%d" % i)
-            if engine == "g":
-                nc.gpsimd.tensor_tensor(inv_t[:], root_t[i][:], root_t[i][:], ALU.mult)
+        def square(i, engine="s", back=False):
+            inv[i] = keep.tile([P, S], F32, name="inv_t%d" % i)
+            if engine == "s":
+                nc.scalar.activation(inv[i][:], root_t[i][:], ACT.Square)
             else:
-                nc.scalar.activation(inv_t[:], root_t[i][:], ACT.Square)
-            inv[i] = psum.tile([P, S], F32, name="inv%d" % i, tag="bank%d" % i)
-            for c in range(4):
-                nc.tensor.transpose(inv[i][:, c * P : (c + 1) * P], inv_t[:, c, :], ident[:])
+                (nc.gpsimd if engine == "g" else nc.vector).tensor_tensor(inv[i][:], root_t[i][:], root_t[i][:], ALU.mult)
 
         def hop_a(i, engines):
             for h in range(2):
                 gather_half(engines[h], a_at[i][:, half_cols(h)], a_sb[i][:], n3_sb, h)
 
         def numer(i, engine="v", cols=slice(0, S)):
-            (nc.gpsimd if engine == "g" else nc.vector).tensor_tensor(num[i][:, cols], a_sb[i][:, cols], a_at[i][:, cols], ALU.subtract)
+            if engine == "g":
+                nc.gpsimd.tensor_tensor(num[i][:, cols], a_sb[i][:, cols], a_at[i][:, cols], ALU.subtract)
+            else:
+                nc.vector.tensor_tensor(num[i][:, cols], acc[0, i][:, cols], a_at[i][:, cols], ALU.subtract)
 
         def finish(i, cols=slice(0, S)):
             res = keep.tile([P, cols.stop - cols.start], F32, name="res%d_%d" % (i, cols.start))
             nc.vector.tensor_tensor(res[:], inv[i][:, cols], num[i][:, cols], ALU.mult)
             nc.sync.dma_start(out[i * P : (i + 1) * P, cols], res[:])
 
-        quantise_z(0)
-        [b_out(i, 0) for i in range(4)]
-        [a_out(i, 0, "s") for i in range(4)]
-        quantise_z(1)
-        [b_out(i, 1) for i in range(4)]
-        a_out(0, 1, "v")
-        a_out(1, 1, "v")
+        y_out(0)
+        y_out(1)
+        cand(1, hc_sb, "w_bf")
+        hop1(0, "sv")
+        diff(0, "g")
+        y_out(2)
+        hop1(1, "sv")
+        diff(1, "g")
+        y_out(3)
+        hop1(2, "sv")
+        hop1(3, "sv")
+        diff(2, "v")
+        diff(3, "v")
+        hop2(0, 0, "s")
+        hop2(1, 0, "s")
+        hop2(2, 0, "v")
+        hop2(3, 0, "s")
+        z_max(0)
+        z_max(1)
+        hop2(0, 1, "s", "y_at3")
+        hop2(1, 1, "s")
+        hop2(2, 1, "s")
+        hop2(3, 1, "s")
+        z_sign(0)
+        z_sign(1)
+        z_quant(0)
+        z_quant(1)
+        score(1, 0, 256)
+        [b_out(i, 0, 256) for i in range(4)]
+        z_max(2, "z_bf0")
+        z_max(3, "z_bf1")
+        z_sign(2)
+        z_sign(3)
+        z_quant(2)
+        z_quant(3)
+        score(1, 256, 512)
+        cand(0, ca_sb, "z_bf3")
+        score(0, 0, 512)
+        [b_out(i, 256, 512) for i in range(4)]
         hop_b(0, "vv")
+        denom(0, "g")
         hop_b(1, "ss")
-        hop_b(2, "vv")
+        denom(1, "g")
+        a_out(0, "v")
+        a_out(1, "s")
+        hop_b(2, "ss")
+        denom(2, "g")
+        a_out(2, "s")
         hop_b(3, "ss")
-        a_out(2, 1, "v")
-        a_out(3, 1, "v")
+        denom(3, "g")
+        a_out(3, "s")
+        hop_a(0, "vv")
+        hop_a(1, "vv")
+        numer(0, "v", half_cols(0))
+        numer(0, "v", half_cols(1))
+        numer(1, "v", half_cols(0))
+        numer(1, "v", half_cols(1))
+        hop_a(2, "vv")
+        numer(2, "v", half_cols(0))
+        numer(2, "v", half_cols(1))
+        hop_a(3, "sv")
         root(0)
         root(1)
-        hop_a(0, "vv")
         square(0)
         square(1)
-        numer(0)
         root(2)
         root(3)
-        hop_a(1, "vv")
-        finish(0)
-        numer(1)
         square(2)
         square(3)
+        finish(0)
+        numer(3)
         finish(1)
-        hop_a(2, "sv")
-        numer(2)
-        hop_a(3, "ss")
         finish(2)
-        numer(3, "v", half_cols(0))
-        numer(3, "v", half_cols(1))
         finish(3, half_cols(0))
         finish(3, half_cols(1))

@@ -46,19 +46,19 @@ def tile_picked_cdhnormbhopmx_none_p_kernel(tc, x_words, x_scales, w1, gs, offs,
             gather(engine, dst, window, offsets, half_cols(h))
 
         offs_sb = load_list(offs, "offs_sb")
-        ca_sb = load_list(ca, "ca_sb")
-        hc_sb = load_list(hc, "hc_sb")
-        warm = keep.tile([P, 1], F32, name="warm")
-        nc.vector.memset(warm[:], 1.0)
-        nc.scalar.activation(warm[:], warm[:], ACT.Abs_reciprocal_sqrt)
         xs = keep.tile([P, T], U8, name="xs")
         for q in range(4):
-            nc.sync.dma_start(
+            (nc.sync if q < 2 else nc.scalar).dma_start(
                 xs[32 * q : 32 * q + 32, :].bitcast(I32),
                 x_scales[0, 4 * q : 4 * q + 4, :].bitcast(I32).partition_broadcast(8),
             )
+        warm = keep.tile([P, 1], F32, name="warm")
+        nc.vector.memset(warm[:], 1.0)
+        nc.scalar.activation(warm[:], warm[:], ACT.Abs_reciprocal_sqrt)
+        ca_sb = load_list(ca, "ca_sb")
         xw = keep.tile([P, T], I32, name="xw")
         nc.sync.dma_start(xw[:], x_words[0].rearrange("p n r -> p (n r)").bitcast(I32))
+        hc_sb = load_list(hc, "hc_sb")
         w_rows = w1.rearrange("(p j) c -> p j c", j=PACK)
         w_raw = []
         for h in range(2):
@@ -93,18 +93,21 @@ def tile_picked_cdhnormbhopmx_none_p_kernel(tc, x_words, x_scales, w1, gs, offs,
 
         w_bf = keep.tile([P, PACK, P, PACK], BF16, name="w_bf", tag="w_bf", align_bytes=64)
 
-        def cast_w(on_vector, m0, m1):
+        def cast_w(engine, m0, m1):
             h = m0 // 64
-            src = w_raw[h][:, :, PACK * (m0 - 64 * h) : PACK * (m1 - 64 * h)].rearrange("p j (m t) -> p m t j", t=PACK)
-            dst = w_bf[:, :, m0:m1, :].rearrange("p t m j -> p m t j")
-            if on_vector:
-                nc.vector.tensor_copy(dst, src)
-            else:
-                nc.scalar.copy(dst, src)
+            src = w_raw[h][:, :, PACK * (m0 - 64 * h) : PACK * (m1 - 64 * h)].rearrange("p j (m t) -> p m j t", t=PACK)
+            dst = w_bf[:, :, m0:m1, :].rearrange("p t m j -> p m j t")
+            for t0 in (0, 2):
+                if engine == "v":
+                    nc.vector.tensor_copy(dst[:, :, :, t0 : t0 + 2], src[:, :, :, t0 : t0 + 2])
+                elif engine == "g":
+                    nc.gpsimd.tensor_scalar(dst[:, :, :, t0 : t0 + 2], src[:, :, :, t0 : t0 + 2], 1.0, 0.0, ALU.mult, ALU.add)
+                else:
+                    nc.scalar.copy(dst[:, :, :, t0 : t0 + 2], src[:, :, :, t0 : t0 + 2])
 
-        cast_w(False, 0, 64)
-        cast_w(False, 64, 88)
-        cast_w(True, 88, 128)
+        cast_w("s", 0, 64)
+        cast_w("s", 64, 88)
+        cast_w("v", 88, 128)
         w_codes = keep.tile([P, PACK, P], U32, name="w_codes", align_bytes=64)
         w_scales = keep.tile([P, PACK, P], U8, name="w_scales", align_bytes=64)
         y_ps = []
@@ -152,10 +155,10 @@ def tile_picked_cdhnormbhopmx_none_p_kernel(tc, x_words, x_scales, w1, gs, offs,
             else:
                 nc.vector.scalar_tensor_tensor(st_all[:, t, :], y_ps[t][:], gs_abs[:, t : t + 1], y_at[t][:], ALU.mult, ALU.subtract)
 
-        def hop2(t, h, engine, tag=None):
+        def hop2(t, h, engine, tag=None, part=slice(0, HALF)):
             if h not in st_at:
                 st_at[h] = keep.tile([P, PACK, HALF], F32, name="st_at%d" % h, tag=tag or "st_at%d" % h, align_bytes=64)
-            gather_half(engine, st_at[h][:, t, :], st_all[:, t, :], n2_sb, h)
+            gather(engine, st_at[h][:, t, part], st_all[:, t, :], n2_sb, slice(h * HALF + part.start, h * HALF + part.stop))
 
         b_abs = [keep.tile([P, S], F32, name="b_abs%d" % i) for i in range(4)]
         a_sb = [keep.tile([P, S], F32, name="a_sb%d" % i) for i in range(4)]
@@ -171,9 +174,9 @@ def tile_picked_cdhnormbhopmx_none_p_kernel(tc, x_words, x_scales, w1, gs, offs,
             z_abs[q] = keep.tile([P, QW, PACK], BF16, name="z_abs%d" % q, tag=tag or "z_abs%d" % q, align_bytes=64)
             cols = slice(q * QW, (q + 1) * QW)
             nc.vector.tensor_tensor(
-                z_abs[q][:].rearrange("p (c i) t -> p c t i", i=4),
-                st_all[:, :, cols].rearrange("p t (c i) -> p c t i", i=4),
-                st_at[q // 2][:, :, (q % 2) * QW : (q % 2 + 1) * QW].rearrange("p t (c i) -> p c t i", i=4),
+                z_abs[q][:].rearrange("p (c i) t -> p c t i", i=2),
+                st_all[:, :, cols].rearrange("p t (c i) -> p c t i", i=2),
+                st_at[q // 2][:, :, (q % 2) * QW : (q % 2 + 1) * QW].rearrange("p t (c i) -> p c t i", i=2),
                 ALU.max,
             )
 
@@ -212,8 +215,8 @@ def tile_picked_cdhnormbhopmx_none_p_kernel(tc, x_words, x_scales, w1, gs, offs,
             else:
                 nc.scalar.copy(a_sb[i][:, c0:c1], acc[0, i][:, c0:c1])
 
-        b_at = [keep.tile([P, S], F32, name="b_at%d" % i) for i in range(4)]
-        a_at = [keep.tile([P, S], F32, name="a_at%d" % i) for i in range(4)]
+        b_at = [keep.tile([P, S], F32, name="b_at%d" % i, tag="b_at%d" % i) for i in range(4)]
+        a_at = {}
         num = [keep.tile([P, S], F32, name="num%d" % i) for i in range(4)]
         den = {}
         root_t = {}
@@ -238,7 +241,8 @@ def tile_picked_cdhnormbhopmx_none_p_kernel(tc, x_words, x_scales, w1, gs, offs,
             else:
                 (nc.gpsimd if engine == "g" else nc.vector).tensor_tensor(inv[i][:], root_t[i][:], root_t[i][:], ALU.mult)
 
-        def hop_a(i, engines):
+        def hop_a(i, engines, tag=None):
+            a_at[i] = keep.tile([P, S], F32, name="a_at%d" % i, tag=tag or "a_at%d" % i)
             for h in range(2):
                 gather_half(engines[h], a_at[i][:, half_cols(h)], a_sb[i][:], n3_sb, h)
 
@@ -248,9 +252,9 @@ def tile_picked_cdhnormbhopmx_none_p_kernel(tc, x_words, x_scales, w1, gs, offs,
             else:
                 nc.vector.tensor_tensor(num[i][:, cols], acc[0, i][:, cols], a_at[i][:, cols], ALU.subtract)
 
-        def finish(i, cols=slice(0, S)):
+        def finish(i, cols=slice(0, S), engine="v"):
             res = keep.tile([P, cols.stop - cols.start], F32, name="res%d_%d" % (i, cols.start))
-            nc.vector.tensor_tensor(res[:], inv[i][:, cols], num[i][:, cols], ALU.mult)
+            (nc.gpsimd if engine == "g" else nc.vector).tensor_tensor(res[:], inv[i][:, cols], num[i][:, cols], ALU.mult)
             nc.sync.dma_start(out[i * P : (i + 1) * P, cols], res[:])
 
         y_out(0)
@@ -261,18 +265,18 @@ def tile_picked_cdhnormbhopmx_none_p_kernel(tc, x_words, x_scales, w1, gs, offs,
         y_out(2)
         hop1(1, "sv")
         diff(1, "g")
-        y_out(3)
+        y_out(3, "v")
         hop1(2, "sv")
         hop1(3, "sv")
         diff(2, "v")
         diff(3, "v")
         hop2(0, 0, "s")
         hop2(1, 0, "s")
-        hop2(2, 0, "v")
-        hop2(3, 0, "s")
+        hop2(2, 0, "s")
+        hop2(3, 0, "v")
         z_max(0)
         z_max(1)
-        hop2(0, 1, "s", "y_at3")
+        hop2(0, 1, "s", "y_at1")
         hop2(1, 1, "s")
         hop2(2, 1, "s")
         hop2(3, 1, "s")
@@ -297,34 +301,32 @@ def tile_picked_cdhnormbhopmx_none_p_kernel(tc, x_words, x_scales, w1, gs, offs,
         hop_b(1, "ss")
         denom(1, "g")
         a_out(0, "v")
-        a_out(1, "s")
         hop_b(2, "ss")
         denom(2, "g")
-        a_out(2, "s")
+        a_out(1, "s")
         hop_b(3, "ss")
         denom(3, "g")
-        a_out(3, "s")
-        hop_a(0, "vv")
-        hop_a(1, "vv")
-        numer(0, "v", half_cols(0))
-        numer(0, "v", half_cols(1))
-        numer(1, "v", half_cols(0))
-        numer(1, "v", half_cols(1))
-        hop_a(2, "vv")
-        numer(2, "v", half_cols(0))
-        numer(2, "v", half_cols(1))
-        hop_a(3, "sv")
         root(0)
-        root(1)
+        hop_a(0, "vv")
+        a_out(2, "v")
+        numer(0)
+        hop_a(1, "vv")
         square(0)
+        root(1)
+        a_out(3, "s")
         square(1)
+        numer(1)
+        finish(0, engine="g")
         root(2)
+        hop_a(2, "vv")
         root(3)
         square(2)
+        numer(2)
+        finish(1, engine="g")
         square(3)
-        finish(0)
-        numer(3)
-        finish(1)
+        hop_a(3, "vv")
         finish(2)
+        numer(3, "v", half_cols(0))
+        numer(3, "v", half_cols(1))
         finish(3, half_cols(0))
         finish(3, half_cols(1))

@@ -17,8 +17,15 @@ ACT = mybir.ActivationFunctionType
 
 P = 128
 PACK = 4
+QUAD = 32
+GROUP = 16
+TILES = C // P
+ALL = slice(0, S)
 HALF = S // 2
-LIST_COLS = S // 16
+HALVES = (slice(0, HALF), slice(HALF, S))
+QUARTER = S // 4
+DEN_OFFSET = 8.0
+PLAIN, HASHED = 0, 1
 
 
 def tile_picked_cdhnormbhopmx_none_p_kernel(tc, x_words, x_scales, w1, gs, offs, n1, n2, ca, hc, n3, n4, out):
@@ -28,43 +35,51 @@ def tile_picked_cdhnormbhopmx_none_p_kernel(tc, x_words, x_scales, w1, gs, offs,
         psum = ctx.enter_context(tc.psum_pool(name="psum", bufs=1))
 
         def load_list(src, name):
-            tile = keep.tile([P, LIST_COLS], U16, name=name)
+            tile = keep.tile([P, S // GROUP], U16, name=name)
             nc.sync.dma_start(tile[:], src)
             return tile
 
-        def half_cols(h):
-            return slice(h * HALF, (h + 1) * HALF)
+        def entries(offsets, cols):
+            return offsets[:, cols.start // GROUP : cols.stop // GROUP]
 
         def gather(engine, dst, window, offsets, cols):
-            picked = window.indirect(offsets[:, cols.start // 16 : cols.stop // 16])
-            if engine == "v":
+            picked = window.indirect(entries(offsets, cols))
+            if engine == "vector":
                 nc.vector.tensor_copy(dst, picked)
             else:
                 nc.scalar.activation(dst, picked, ACT.Copy)
 
-        def gather_half(engine, dst, window, offsets, h):
-            gather(engine, dst, window, offsets, half_cols(h))
+        def mx_product(dst, lhs_words, lhs_scales, rhs_words, rhs_scales):
+            nc.tensor.matmul_mx(
+                out=dst,
+                lhsT=lhs_words.bitcast(FP8X4),
+                lhsT_scale=lhs_scales,
+                rhs=rhs_words.bitcast(FP8X4),
+                rhs_scale=rhs_scales,
+                start=True,
+                stop=True,
+            )
 
         offs_sb = load_list(offs, "offs_sb")
         xs = keep.tile([P, T], U8, name="xs")
-        for q in range(4):
-            (nc.sync if q < 2 else nc.scalar).dma_start(
-                xs[32 * q : 32 * q + 32, :].bitcast(I32),
-                x_scales[0, 4 * q : 4 * q + 4, :].bitcast(I32).partition_broadcast(8),
+        for q in range(P // QUAD):
+            nc.sync.dma_start(
+                xs[QUAD * q : QUAD * (q + 1), :].bitcast(I32),
+                x_scales[0, 4 * q : 4 * q + 4, :].bitcast(I32).partition_broadcast(QUAD // 4),
             )
         warm = keep.tile([P, 1], F32, name="warm")
         nc.vector.memset(warm[:], 1.0)
         nc.scalar.activation(warm[:], warm[:], ACT.Abs_reciprocal_sqrt)
         ca_sb = load_list(ca, "ca_sb")
-        xw = keep.tile([P, T], I32, name="xw")
-        nc.sync.dma_start(xw[:], x_words[0].rearrange("p n r -> p (n r)").bitcast(I32))
-        hc_sb = load_list(hc, "hc_sb")
         w_rows = w1.rearrange("(p j) c -> p j c", j=PACK)
         w_raw = []
         for h in range(2):
             raw = keep.tile([P, PACK, H // 2], F32, name="w_raw%d" % h)
             nc.sync.dma_start(raw[:], w_rows[:, :, h * H // 2 : (h + 1) * H // 2])
             w_raw.append(raw)
+        hc_sb = load_list(hc, "hc_sb")
+        xw = keep.tile([P, T], I32, name="xw")
+        nc.sync.dma_start(xw[:], x_words[0].rearrange("p n r -> p (n r)").bitcast(I32))
         n1_sb = load_list(n1, "n1_sb")
         n2_sb = load_list(n2, "n2_sb")
         gs_sb = keep.tile([P, PACK], F32, name="gs_sb")
@@ -76,257 +91,178 @@ def tile_picked_cdhnormbhopmx_none_p_kernel(tc, x_words, x_scales, w1, gs, offs,
         nc.scalar.activation(gs_abs[:], gs_sb[:], ACT.Abs)
         gs_sign = keep.tile([P, PACK], BF16, name="gs_sign")
         nc.scalar.activation(gs_sign[:], gs_sb[:], ACT.Sign)
+
         hc_scales = keep.tile([P, C], U8, name="hc_scales", align_bytes=64)
         nc.gpsimd.memset(hc_scales[:], 0)
-
         tok_scales = keep.tile([P, S], U8, name="tok_scales", align_bytes=64)
-        tok_words = keep.tile([P, S], U32, name="tok_words", align_bytes=64)
         ca_scales = keep.tile([P, C], U8, name="ca_scales", align_bytes=64)
         hc_picked = keep.tile([P, C], U8, name="hc_picked", align_bytes=64)
         nc.vector.tensor_copy(tok_scales[:], xs[:].indirect(offs_sb[:]))
-        nc.vector.tensor_copy(tok_words[:], xw[:].bitcast(U32).indirect(offs_sb[:]))
         nc.vector.tensor_copy(ca_scales[:], xs[:].indirect(ca_sb[:]))
         nc.vector.tensor_copy(hc_picked[:], xs[:].indirect(hc_sb[:]))
         for r in range(4):
-            first = r if r < 2 else 16 + r
-            nc.sync.dma_start(hc_scales[r:P:32, :].bitcast(I32), hc_picked[first:P:32, :].bitcast(I32))
+            first = r + GROUP * (r // 2)
+            nc.sync.dma_start(hc_scales[r:P:QUAD, :].bitcast(I32), hc_picked[first:P:QUAD, :].bitcast(I32))
 
-        w_bf = keep.tile([P, PACK, P, PACK], BF16, name="w_bf", tag="w_bf", align_bytes=64)
-
-        def cast_w(engine, m0, m1):
-            h = m0 // 64
-            src = w_raw[h][:, :, PACK * (m0 - 64 * h) : PACK * (m1 - 64 * h)].rearrange("p j (m t) -> p m j t", t=PACK)
-            dst = w_bf[:, :, m0:m1, :].rearrange("p t m j -> p m j t")
+        w_bf = keep.tile([P, PACK, P, PACK], BF16, name="w_bf", align_bytes=64)
+        for h in range(2):
+            src = w_raw[h][:].rearrange("p j (m t) -> p m j t", t=PACK)
+            dst = w_bf[:, :, h * P // 2 : (h + 1) * P // 2, :].rearrange("p t m j -> p m j t")
             for t0 in (0, 2):
-                if engine == "v":
-                    nc.vector.tensor_copy(dst[:, :, :, t0 : t0 + 2], src[:, :, :, t0 : t0 + 2])
-                elif engine == "g":
-                    nc.gpsimd.tensor_scalar(dst[:, :, :, t0 : t0 + 2], src[:, :, :, t0 : t0 + 2], 1.0, 0.0, ALU.mult, ALU.add)
-                else:
-                    nc.scalar.copy(dst[:, :, :, t0 : t0 + 2], src[:, :, :, t0 : t0 + 2])
-
-        cast_w("s", 0, 64)
-        cast_w("s", 64, 88)
-        cast_w("v", 88, 128)
+                nc.scalar.copy(dst[:, :, :, t0 : t0 + 2], src[:, :, :, t0 : t0 + 2])
         w_codes = keep.tile([P, PACK, P], U32, name="w_codes", align_bytes=64)
         w_scales = keep.tile([P, PACK, P], U8, name="w_scales", align_bytes=64)
-        y_ps = []
         for t in range(PACK):
             nc.vector.quantize_mx(
                 out=w_codes[:, t, :].bitcast(FP8X4),
                 scales=w_scales[:, t, :],
                 in_=w_bf[:, t, :, :].rearrange("p m j -> p (m j)"),
             )
-            acc = psum.tile([P, S], F32, name="y_ps%d" % t, tag="bank%d" % t)
-            nc.tensor.matmul_mx(
-                out=acc[:],
-                lhsT=w_codes[:, t, :].bitcast(FP8X4),
-                lhsT_scale=w_scales[:, t, :],
-                rhs=tok_words[:].bitcast(FP8X4),
-                rhs_scale=tok_scales[:],
-                start=True,
-                stop=True,
-            )
-            y_ps.append(acc)
 
-        cand_words = {}
-        y_sb = [keep.tile([P, S], F32, name="y_sb%d" % t, tag="y_sb%d" % t, align_bytes=64) for t in range(PACK)]
+        tok_words = keep.tile([P, S], U32, name="tok_words", align_bytes=64)
+        for cols in HALVES:
+            nc.vector.tensor_copy(tok_words[:, cols], xw[:].bitcast(U32).indirect(entries(offs_sb, cols)))
+        y_ps = [psum.tile([P, S], F32, name="y_ps%d" % t, tag="bank%d" % t) for t in range(PACK)]
+        y_sb = [keep.tile([P, S], F32, name="y_sb%d" % t, align_bytes=64) for t in range(PACK)]
         y_at = [keep.tile([P, S], F32, name="y_at%d" % t, tag="y_at%d" % t, align_bytes=64) for t in range(PACK)]
-        st_all = keep.tile([P, PACK, S], F32, name="st_all")
-        st_at = {}
+        st = keep.tile([P, PACK, S], F32, name="st")
 
-        def cand(which, lst, tag):
-            cand_words[which] = keep.tile([P, C], U32, name="cand_words%d" % which, tag=tag, align_bytes=64)
-            nc.vector.tensor_copy(cand_words[which][:], xw[:].bitcast(U32).indirect(lst[:]))
+        def empty_y(t, cols):
+            nc.scalar.activation(y_sb[t][:, cols], y_ps[t][:, cols], ACT.Identity, scale=gs_abs[:, t : t + 1])
 
-        def y_out(t, engine="s"):
-            if engine == "s":
-                nc.scalar.activation(y_sb[t][:], y_ps[t][:], ACT.Identity, scale=gs_abs[:, t : t + 1])
+        early = 2
+        for cols in HALVES:
+            for t in range(PACK):
+                mx_product(y_ps[t][:, cols], w_codes[:, t, :], w_scales[:, t, :], tok_words[:, cols], tok_scales[:, cols])
+            for t in range(early):
+                empty_y(t, cols)
+
+        cand_scales = {PLAIN: ca_scales, HASHED: hc_scales}
+        cand_words = {}
+
+        def pick_candidates(kind, offsets, tag):
+            cand_words[kind] = keep.tile([P, C], U32, name="cand_words%d" % kind, tag=tag, align_bytes=64)
+            nc.vector.tensor_copy(cand_words[kind][:], xw[:].bitcast(U32).indirect(offsets[:]))
+
+        pick_candidates(HASHED, hc_sb, "hc_words")
+
+        for t in range(PACK):
+            gather("scalar", y_at[t][:, HALVES[0]], y_sb[t][:], n1_sb, HALVES[0])
+            gather("vector", y_at[t][:, HALVES[1]], y_sb[t][:], n1_sb, HALVES[1])
+            if t == 0:
+                nc.gpsimd.tensor_tensor(st[:, t, :], y_sb[t][:], y_at[t][:], ALU.subtract)
             else:
-                nc.vector.tensor_scalar(y_sb[t][:], y_ps[t][:], gs_abs[:, t : t + 1], None, ALU.mult)
+                nc.vector.scalar_tensor_tensor(
+                    st[:, t, :], y_ps[t][:], gs_abs[:, t : t + 1], y_at[t][:], ALU.mult, ALU.subtract
+                )
+            if t + early < PACK:
+                empty_y(t + early, ALL)
 
-        def hop1(t, engines):
-            for h in range(2):
-                gather_half(engines[h], y_at[t][:, half_cols(h)], y_sb[t][:], n1_sb, h)
-
-        def diff(t, engine="v"):
-            if engine == "g":
-                nc.gpsimd.tensor_tensor(st_all[:, t, :], y_sb[t][:], y_at[t][:], ALU.subtract)
-            else:
-                nc.vector.scalar_tensor_tensor(st_all[:, t, :], y_ps[t][:], gs_abs[:, t : t + 1], y_at[t][:], ALU.mult, ALU.subtract)
-
-        def hop2(t, h, engine, tag=None, part=slice(0, HALF)):
-            if h not in st_at:
-                st_at[h] = keep.tile([P, PACK, HALF], F32, name="st_at%d" % h, tag=tag or "st_at%d" % h, align_bytes=64)
-            gather(engine, st_at[h][:, t, part], st_all[:, t, :], n2_sb, slice(h * HALF + part.start, h * HALF + part.stop))
-
-        b_abs = [keep.tile([P, S], F32, name="b_abs%d" % i) for i in range(4)]
-        a_sb = [keep.tile([P, S], F32, name="a_sb%d" % i) for i in range(4)]
         z_codes = keep.tile([P, S], U32, name="z_codes", align_bytes=64)
         z_scales = keep.tile([P, S], U8, name="z_scales", align_bytes=64)
-        QW = S // 4
-        sign_wide = gs_sign[:].unsqueeze(1).to_broadcast([P, QW, PACK])
+        sign_wide = gs_sign[:].unsqueeze(1).to_broadcast([P, QUARTER, PACK])
+        b_abs = [keep.tile([P, S], F32, name="b_abs%d" % i) for i in range(TILES)]
+        st_at = {}
         z_abs = {}
-        z_bf = {}
         acc = {}
 
-        def z_max(q, tag=None):
-            z_abs[q] = keep.tile([P, QW, PACK], BF16, name="z_abs%d" % q, tag=tag or "z_abs%d" % q, align_bytes=64)
-            cols = slice(q * QW, (q + 1) * QW)
+        def gather_st(h, tag, on_vector):
+            st_at[h] = keep.tile([P, PACK, HALF], F32, name="st_at%d" % h, tag=tag, align_bytes=64)
+            for t in range(PACK):
+                gather("vector" if t == on_vector else "scalar", st_at[h][:, t, :], st[:, t, :], n2_sb, HALVES[h])
+
+        def quarter(u):
+            return slice(u * QUARTER, (u + 1) * QUARTER)
+
+        def largest(u, tag):
+            z_abs[u] = keep.tile([P, QUARTER, PACK], BF16, name="z_abs%d" % u, tag=tag, align_bytes=64)
             nc.vector.tensor_tensor(
-                z_abs[q][:].rearrange("p (c i) t -> p c t i", i=2),
-                st_all[:, :, cols].rearrange("p t (c i) -> p c t i", i=2),
-                st_at[q // 2][:, :, (q % 2) * QW : (q % 2 + 1) * QW].rearrange("p t (c i) -> p c t i", i=2),
+                z_abs[u][:].rearrange("p (c i) t -> p c t i", i=2),
+                st[:, :, quarter(u)].rearrange("p t (c i) -> p c t i", i=2),
+                st_at[u // 2][:, :, quarter(u % 2)].rearrange("p t (c i) -> p c t i", i=2),
                 ALU.max,
             )
 
-        def z_sign(q):
-            z_bf[q] = keep.tile([P, QW, PACK], BF16, name="z_bf%d" % q, tag="z_bf%d" % q, align_bytes=64)
-            nc.vector.tensor_tensor(z_bf[q][:], z_abs[q][:], sign_wide, ALU.mult)
-
-        def z_quant(q):
-            cols = slice(q * QW, (q + 1) * QW)
-            nc.vector.quantize_mx(
-                out=z_codes[:, cols].bitcast(FP8X4), scales=z_scales[:, cols], in_=z_bf[q][:].rearrange("p n t -> p (n t)")
-            )
-
-        def score(which, c0, c1):
-            scales = hc_scales if which == 1 else ca_scales
-            for i in range(4):
-                if (which, i) not in acc:
-                    acc[which, i] = psum.tile([P, S], F32, name="sc%d%d" % (which, i), tag="bank%d" % (4 * which + i))
-                rows = slice(i * P, (i + 1) * P)
-                nc.tensor.matmul_mx(
-                    out=acc[which, i][:, c0:c1],
-                    lhsT=cand_words[which][:, rows].bitcast(FP8X4),
-                    lhsT_scale=scales[:, rows],
-                    rhs=z_codes[:, c0:c1].bitcast(FP8X4),
-                    rhs_scale=z_scales[:, c0:c1],
-                    start=True,
-                    stop=True,
+        def quantise_z(h):
+            z_bf = {}
+            for u in (2 * h, 2 * h + 1):
+                z_bf[u] = keep.tile([P, QUARTER, PACK], BF16, name="z_bf%d" % u, tag="z_bf%d" % u, align_bytes=64)
+                nc.vector.tensor_tensor(z_bf[u][:], z_abs[u][:], sign_wide, ALU.mult)
+            for u in (2 * h, 2 * h + 1):
+                nc.vector.quantize_mx(
+                    out=z_codes[:, quarter(u)].bitcast(FP8X4),
+                    scales=z_scales[:, quarter(u)],
+                    in_=z_bf[u][:].rearrange("p n t -> p (n t)"),
                 )
 
-        def b_out(i, c0, c1):
-            nc.scalar.activation(b_abs[i][:, c0:c1], acc[1, i][:, c0:c1], ACT.Abs)
+        def score(kind, cols):
+            for i in range(TILES):
+                if (kind, i) not in acc:
+                    bank = "bank%d" % (TILES * kind + i)
+                    acc[kind, i] = psum.tile([P, S], F32, name="acc%d_%d" % (kind, i), tag=bank)
+                rows = slice(i * P, (i + 1) * P)
+                mx_product(
+                    acc[kind, i][:, cols],
+                    cand_words[kind][:, rows],
+                    cand_scales[kind][:, rows],
+                    z_codes[:, cols],
+                    z_scales[:, cols],
+                )
 
-        def a_out(i, engine, c0=0, c1=S):
-            if engine == "v":
-                nc.vector.tensor_copy(a_sb[i][:, c0:c1], acc[0, i][:, c0:c1])
+        def empty_b(cols):
+            for i in range(TILES):
+                nc.scalar.activation(b_abs[i][:, cols], acc[HASHED, i][:, cols], ACT.Abs)
+
+        gather_st(0, "st_at0", on_vector=2)
+        largest(0, "z_abs0")
+        largest(1, "z_abs1")
+        gather_st(1, "y_at%d" % (PACK - 1), on_vector=None)
+        quantise_z(0)
+        score(HASHED, HALVES[0])
+        empty_b(HALVES[0])
+        largest(2, "z_bf0")
+        largest(3, "z_bf1")
+        quantise_z(1)
+        score(HASHED, HALVES[1])
+        pick_candidates(PLAIN, ca_sb, "z_bf3")
+        score(PLAIN, ALL)
+        empty_b(HALVES[1])
+
+        a_sb = [keep.tile([P, S], F32, name="a_sb%d" % i) for i in range(TILES)]
+
+        def empty_a(i):
+            if i % 2 == 0:
+                nc.vector.tensor_copy(a_sb[i][:], acc[PLAIN, i][:])
             else:
-                nc.scalar.copy(a_sb[i][:, c0:c1], acc[0, i][:, c0:c1])
+                nc.scalar.copy(a_sb[i][:], acc[PLAIN, i][:])
 
-        b_at = [keep.tile([P, S], F32, name="b_at%d" % i, tag="b_at%d" % i) for i in range(4)]
-        a_at = {}
-        num = [keep.tile([P, S], F32, name="num%d" % i) for i in range(4)]
-        den = {}
-        root_t = {}
-        inv = {}
+        den = []
+        for i in range(TILES):
+            b_at = keep.tile([P, S], F32, name="b_at%d" % i)
+            for cols in HALVES:
+                gather("vector" if i == 0 else "scalar", b_at[:, cols], b_abs[i][:], n4_sb, cols)
+            den.append(keep.tile([P, S], F32, name="den%d" % i))
+            nc.gpsimd.tensor_tensor(den[i][:], b_abs[i][:], b_at[:], ALU.add)
+            if i > 0:
+                empty_a(i - 1)
 
-        def hop_b(i, engines):
-            for h in range(2):
-                gather_half(engines[h], b_at[i][:, half_cols(h)], b_abs[i][:], n4_sb, h)
-
-        def denom(i, engine):
-            den[i] = keep.tile([P, S], F32, name="den%d" % i)
-            (nc.gpsimd if engine == "g" else nc.vector).tensor_tensor(den[i][:], b_abs[i][:], b_at[i][:], ALU.add)
-
-        def root(i):
-            root_t[i] = keep.tile([P, S], F32, name="root_t%d" % i)
-            nc.scalar.activation(root_t[i][:], den[i][:], ACT.Abs_reciprocal_sqrt, bias=8.0)
-
-        def square(i, engine="s", back=False):
-            inv[i] = keep.tile([P, S], F32, name="inv_t%d" % i)
-            if engine == "s":
-                nc.scalar.activation(inv[i][:], root_t[i][:], ACT.Square)
-            else:
-                (nc.gpsimd if engine == "g" else nc.vector).tensor_tensor(inv[i][:], root_t[i][:], root_t[i][:], ALU.mult)
-
-        def hop_a(i, engines, tag=None):
-            a_at[i] = keep.tile([P, S], F32, name="a_at%d" % i, tag=tag or "a_at%d" % i)
-            for h in range(2):
-                gather_half(engines[h], a_at[i][:, half_cols(h)], a_sb[i][:], n3_sb, h)
-
-        def numer(i, engine="v", cols=slice(0, S)):
-            if engine == "g":
-                nc.gpsimd.tensor_tensor(num[i][:, cols], a_sb[i][:, cols], a_at[i][:, cols], ALU.subtract)
-            else:
-                nc.vector.tensor_tensor(num[i][:, cols], acc[0, i][:, cols], a_at[i][:, cols], ALU.subtract)
-
-        def finish(i, cols=slice(0, S), engine="v"):
-            res = keep.tile([P, cols.stop - cols.start], F32, name="res%d_%d" % (i, cols.start))
-            (nc.gpsimd if engine == "g" else nc.vector).tensor_tensor(res[:], inv[i][:, cols], num[i][:, cols], ALU.mult)
-            nc.sync.dma_start(out[i * P : (i + 1) * P, cols], res[:])
-
-        y_out(0)
-        y_out(1)
-        cand(1, hc_sb, "w_bf")
-        hop1(0, "sv")
-        diff(0, "g")
-        y_out(2)
-        hop1(1, "sv")
-        diff(1, "g")
-        y_out(3, "v")
-        hop1(2, "sv")
-        hop1(3, "sv")
-        diff(2, "v")
-        diff(3, "v")
-        hop2(0, 0, "s")
-        hop2(1, 0, "s")
-        hop2(2, 0, "s")
-        hop2(3, 0, "v")
-        z_max(0)
-        z_max(1)
-        hop2(0, 1, "s", "y_at1")
-        hop2(1, 1, "s")
-        hop2(2, 1, "s")
-        hop2(3, 1, "s")
-        z_sign(0)
-        z_sign(1)
-        z_quant(0)
-        z_quant(1)
-        score(1, 0, 256)
-        [b_out(i, 0, 256) for i in range(4)]
-        z_max(2, "z_bf0")
-        z_max(3, "z_bf1")
-        z_sign(2)
-        z_sign(3)
-        z_quant(2)
-        z_quant(3)
-        score(1, 256, 512)
-        cand(0, ca_sb, "z_bf3")
-        score(0, 0, 512)
-        [b_out(i, 256, 512) for i in range(4)]
-        hop_b(0, "vv")
-        denom(0, "g")
-        hop_b(1, "ss")
-        denom(1, "g")
-        a_out(0, "v")
-        hop_b(2, "ss")
-        denom(2, "g")
-        a_out(1, "s")
-        hop_b(3, "ss")
-        denom(3, "g")
-        root(0)
-        hop_a(0, "vv")
-        a_out(2, "v")
-        numer(0)
-        hop_a(1, "vv")
-        square(0)
-        root(1)
-        a_out(3, "s")
-        square(1)
-        numer(1)
-        finish(0, engine="g")
-        root(2)
-        hop_a(2, "vv")
-        root(3)
-        square(2)
-        numer(2)
-        finish(1, engine="g")
-        square(3)
-        hop_a(3, "vv")
-        finish(2)
-        numer(3, "v", half_cols(0))
-        numer(3, "v", half_cols(1))
-        finish(3, half_cols(0))
-        finish(3, half_cols(1))
+        last = TILES - 1
+        for i in range(TILES):
+            root = keep.tile([P, S], F32, name="root%d" % i)
+            nc.scalar.activation(root[:], den[i][:], ACT.Abs_reciprocal_sqrt, bias=DEN_OFFSET)
+            a_at = keep.tile([P, S], F32, name="a_at%d" % i)
+            for cols in HALVES:
+                gather("vector", a_at[:, cols], a_sb[i][:], n3_sb, cols)
+            inv = keep.tile([P, S], F32, name="inv%d" % i)
+            nc.scalar.activation(inv[:], root[:], ACT.Square)
+            if i + 2 == last:
+                empty_a(last)
+            parts = HALVES if i == last else (ALL,)
+            num = keep.tile([P, S], F32, name="num%d" % i)
+            for cols in parts:
+                nc.vector.tensor_tensor(num[:, cols], acc[PLAIN, i][:, cols], a_at[:, cols], ALU.subtract)
+            finisher = nc.gpsimd if i < TILES // 2 else nc.vector
+            for cols in parts:
+                res = keep.tile([P, cols.stop - cols.start], F32, name="res%d_%d" % (i, cols.start))
+                finisher.tensor_tensor(res[:], inv[:, cols], num[:, cols], ALU.mult)
+                nc.sync.dma_start(out[i * P : (i + 1) * P, cols], res[:])

@@ -140,11 +140,14 @@ def tile_picked_cdhnormbhopmx_none_p_kernel(tc, x_words, x_scales, w1, gs, offs,
         cand_scales = {PLAIN: ca_scales, HASHED: hc_scales}
         cand_words = {}
 
-        def pick_candidates(kind, offsets, tag):
-            cand_words[kind] = keep.tile([P, C], U32, name="cand_words%d" % kind, tag=tag, align_bytes=64)
-            nc.vector.tensor_copy(cand_words[kind][:], xw[:].bitcast(U32).indirect(offsets[:]))
+        def pick_candidates(kind, offsets, part, tag):
+            width = part.stop - part.start
+            words = keep.tile([P, width], U32, name="words%d_%d" % (kind, part.start), tag=tag, align_bytes=64)
+            nc.vector.tensor_copy(words[:], xw[:].bitcast(U32).indirect(entries(offsets, part)))
+            for i in range(width // P):
+                cand_words[kind, part.start // P + i] = words[:, i * P : (i + 1) * P]
 
-        pick_candidates(HASHED, hc_sb, "hc_words")
+        pick_candidates(HASHED, hc_sb, ALL, "hc_words")
 
         for t in range(PACK):
             gather("scalar", y_at[t][:, HALVES[0]], y_sb[t][:], n1_sb, HALVES[0])
@@ -162,6 +165,9 @@ def tile_picked_cdhnormbhopmx_none_p_kernel(tc, x_words, x_scales, w1, gs, offs,
         z_scales = keep.tile([P, S], U8, name="z_scales", align_bytes=64)
         sign_wide = gs_sign[:].unsqueeze(1).to_broadcast([P, QUARTER, PACK])
         b_abs = [keep.tile([P, S], F32, name="b_abs%d" % i) for i in range(TILES)]
+        a_sb = [keep.tile([P, S], F32, name="a_sb%d" % i) for i in range(TILES)]
+        first_tiles = range(TILES // 2)
+        other_tiles = range(TILES // 2, TILES)
         st_at = {}
         z_abs = {}
         acc = {}
@@ -195,15 +201,15 @@ def tile_picked_cdhnormbhopmx_none_p_kernel(tc, x_words, x_scales, w1, gs, offs,
                     in_=z_bf[u][:].rearrange("p n t -> p (n t)"),
                 )
 
-        def score(kind, cols):
-            for i in range(TILES):
+        def score(kind, cols, tiles=range(TILES)):
+            for i in tiles:
                 if (kind, i) not in acc:
                     bank = "bank%d" % (TILES * kind + i)
                     acc[kind, i] = psum.tile([P, S], F32, name="acc%d_%d" % (kind, i), tag=bank)
                 rows = slice(i * P, (i + 1) * P)
                 mx_product(
                     acc[kind, i][:, cols],
-                    cand_words[kind][:, rows],
+                    cand_words[kind, i],
                     cand_scales[kind][:, rows],
                     z_codes[:, cols],
                     z_scales[:, cols],
@@ -214,27 +220,31 @@ def tile_picked_cdhnormbhopmx_none_p_kernel(tc, x_words, x_scales, w1, gs, offs,
                 nc.scalar.activation(b_abs[i][:, cols], acc[HASHED, i][:, cols], ACT.Abs)
 
         gather_st(0, "st_at0", on_vector=2)
+        pick_candidates(PLAIN, ca_sb, HALVES[0], "y_at%d" % (PACK - 2))
         largest(0, "z_abs0")
         largest(1, "z_abs1")
         gather_st(1, "y_at%d" % (PACK - 1), on_vector=None)
         quantise_z(0)
         score(HASHED, HALVES[0])
+        score(PLAIN, HALVES[0], first_tiles)
         empty_b(HALVES[0])
+        for i in first_tiles:
+            nc.scalar.copy(a_sb[i][:, HALVES[0]], acc[PLAIN, i][:, HALVES[0]])
         largest(2, "z_bf0")
         largest(3, "z_bf1")
         quantise_z(1)
         score(HASHED, HALVES[1])
-        pick_candidates(PLAIN, ca_sb, "z_bf3")
-        score(PLAIN, ALL)
+        score(PLAIN, HALVES[1], first_tiles)
+        pick_candidates(PLAIN, ca_sb, HALVES[1], "z_bf3")
+        score(PLAIN, ALL, other_tiles)
         empty_b(HALVES[1])
 
-        a_sb = [keep.tile([P, S], F32, name="a_sb%d" % i) for i in range(TILES)]
-
         def empty_a(i):
+            cols = HALVES[1] if i in first_tiles else ALL
             if i % 2 == 0:
-                nc.vector.tensor_copy(a_sb[i][:], acc[PLAIN, i][:])
+                nc.vector.tensor_copy(a_sb[i][:, cols], acc[PLAIN, i][:, cols])
             else:
-                nc.scalar.copy(a_sb[i][:], acc[PLAIN, i][:])
+                nc.scalar.copy(a_sb[i][:, cols], acc[PLAIN, i][:, cols])
 
         den = []
         for i in range(TILES):
@@ -261,7 +271,7 @@ def tile_picked_cdhnormbhopmx_none_p_kernel(tc, x_words, x_scales, w1, gs, offs,
             num = keep.tile([P, S], F32, name="num%d" % i)
             for cols in parts:
                 nc.vector.tensor_tensor(num[:, cols], acc[PLAIN, i][:, cols], a_at[:, cols], ALU.subtract)
-            finisher = nc.gpsimd if i < TILES // 2 else nc.vector
+            finisher = nc.gpsimd if i in first_tiles else nc.vector
             for cols in parts:
                 res = keep.tile([P, cols.stop - cols.start], F32, name="res%d_%d" % (i, cols.start))
                 finisher.tensor_tensor(res[:], inv[:, cols], num[:, cols], ALU.mult)

from contextlib import ExitStack

import concourse.mybir as mybir

K, T, S, H, C = 512, 2048, 512, 512, 512
FLOPS = 2 * K * H * S + 2 * 2 * K * C * S

F32 = mybir.dt.float32
BF16 = mybir.dt.bfloat16
I32 = mybir.dt.int32
U32 = mybir.dt.uint32
U16 = mybir.dt.uint16
U8 = mybir.dt.uint8
FP8X4 = mybir.dt.float8_e4m3fn_x4
ALU = mybir.AluOpType
ACT = mybir.ActivationFunctionType

P = 128
PACK = 4
QUAD = 32
GROUP = 16
TILES = C // P
ALL = slice(0, S)
HALF = S // 2
HALVES = (slice(0, HALF), slice(HALF, S))
QUARTER = S // 4
DEN_OFFSET = 8.0
PLAIN, HASHED = 0, 1


def tile_picked_cdhnormbhopmx_none_p_kernel(tc, x_words, x_scales, w1, gs, offs, n1, n2, ca, hc, n3, n4, out):
    nc = tc.nc
    with ExitStack() as ctx:
        keep = ctx.enter_context(tc.tile_pool(name="keep", bufs=1))
        psum = ctx.enter_context(tc.psum_pool(name="psum", bufs=1))

        def load_list(src, name):
            tile = keep.tile([P, S // GROUP], U16, name=name)
            nc.sync.dma_start(tile[:], src)
            return tile

        def entries(offsets, cols):
            return offsets[:, cols.start // GROUP : cols.stop // GROUP]

        def gather(engine, dst, window, offsets, cols):
            picked = window.indirect(entries(offsets, cols))
            if engine == "vector":
                nc.vector.tensor_copy(dst, picked)
            else:
                nc.scalar.activation(dst, picked, ACT.Copy)

        def mx_product(dst, lhs_words, lhs_scales, rhs_words, rhs_scales):
            nc.tensor.matmul_mx(
                out=dst,
                lhsT=lhs_words.bitcast(FP8X4),
                lhsT_scale=lhs_scales,
                rhs=rhs_words.bitcast(FP8X4),
                rhs_scale=rhs_scales,
                start=True,
                stop=True,
            )

        offs_sb = load_list(offs, "offs_sb")
        xs = keep.tile([P, T], U8, name="xs")
        for q in range(P // QUAD):
            nc.sync.dma_start(
                xs[QUAD * q : QUAD * (q + 1), :].bitcast(I32),
                x_scales[0, 4 * q : 4 * q + 4, :].bitcast(I32).partition_broadcast(QUAD // 4),
            )
        warm = keep.tile([P, 1], F32, name="warm")
        nc.vector.memset(warm[:], 1.0)
        nc.scalar.activation(warm[:], warm[:], ACT.Abs_reciprocal_sqrt)
        ca_sb = load_list(ca, "ca_sb")
        w_rows = w1.rearrange("(p j) c -> p j c", j=PACK)
        w_raw = []
        for h in range(2):
            raw = keep.tile([P, PACK, H // 2], F32, name="w_raw%d" % h)
            nc.sync.dma_start(raw[:], w_rows[:, :, h * H // 2 : (h + 1) * H // 2])
            w_raw.append(raw)
        hc_sb = load_list(hc, "hc_sb")
        xw = keep.tile([P, T], I32, name="xw")
        nc.sync.dma_start(xw[:], x_words[0].rearrange("p n r -> p (n r)").bitcast(I32))
        n1_sb = load_list(n1, "n1_sb")
        n2_sb = load_list(n2, "n2_sb")
        gs_sb = keep.tile([P, PACK], F32, name="gs_sb")
        nc.sync.dma_start(gs_sb[:], gs.rearrange("(p t) o -> p (t o)", t=PACK))
        n4_sb = load_list(n4, "n4_sb")
        n3_sb = load_list(n3, "n3_sb")

        gs_abs = keep.tile([P, PACK], F32, name="gs_abs")
        nc.scalar.activation(gs_abs[:], gs_sb[:], ACT.Abs)
        gs_sign = keep.tile([P, PACK], BF16, name="gs_sign")
        nc.scalar.activation(gs_sign[:], gs_sb[:], ACT.Sign)

        hc_scales = keep.tile([P, C], U8, name="hc_scales", align_bytes=64)
        nc.gpsimd.memset(hc_scales[:], 0)
        tok_scales = keep.tile([P, S], U8, name="tok_scales", align_bytes=64)
        ca_scales = keep.tile([P, C], U8, name="ca_scales", align_bytes=64)
        hc_picked = keep.tile([P, C], U8, name="hc_picked", align_bytes=64)
        nc.vector.tensor_copy(tok_scales[:], xs[:].indirect(offs_sb[:]))
        nc.vector.tensor_copy(ca_scales[:], xs[:].indirect(ca_sb[:]))
        nc.vector.tensor_copy(hc_picked[:], xs[:].indirect(hc_sb[:]))
        for r in range(4):
            first = r + GROUP * (r // 2)
            nc.sync.dma_start(hc_scales[r:P:QUAD, :].bitcast(I32), hc_picked[first:P:QUAD, :].bitcast(I32))

        w_bf = keep.tile([P, PACK, P, PACK], BF16, name="w_bf", align_bytes=64)
        for h in range(2):
            src = w_raw[h][:].rearrange("p j (m t) -> p m j t", t=PACK)
            dst = w_bf[:, :, h * P // 2 : (h + 1) * P // 2, :].rearrange("p t m j -> p m j t")
            for t0 in (0, 2):
                nc.scalar.copy(dst[:, :, :, t0 : t0 + 2], src[:, :, :, t0 : t0 + 2])
        w_codes = keep.tile([P, PACK, P], U32, name="w_codes", align_bytes=64)
        w_scales = keep.tile([P, PACK, P], U8, name="w_scales", align_bytes=64)
        for t in range(PACK):
            nc.vector.quantize_mx(
                out=w_codes[:, t, :].bitcast(FP8X4),
                scales=w_scales[:, t, :],
                in_=w_bf[:, t, :, :].rearrange("p m j -> p (m j)"),
            )

        tok_words = keep.tile([P, S], U32, name="tok_words", align_bytes=64)
        for cols in HALVES:
            nc.vector.tensor_copy(tok_words[:, cols], xw[:].bitcast(U32).indirect(entries(offs_sb, cols)))
        y_ps = [psum.tile([P, S], F32, name="y_ps%d" % t, tag="bank%d" % t) for t in range(PACK)]
        y_sb = [keep.tile([P, S], F32, name="y_sb%d" % t, align_bytes=64) for t in range(PACK)]
        y_at = [keep.tile([P, S], F32, name="y_at%d" % t, tag="y_at%d" % t, align_bytes=64) for t in range(PACK)]
        st = keep.tile([P, PACK, S], F32, name="st")

        def empty_y(t, cols):
            nc.scalar.activation(y_sb[t][:, cols], y_ps[t][:, cols], ACT.Identity, scale=gs_abs[:, t : t + 1])

        early = 2
        for cols in HALVES:
            for t in range(PACK):
                mx_product(y_ps[t][:, cols], w_codes[:, t, :], w_scales[:, t, :], tok_words[:, cols], tok_scales[:, cols])
            for t in range(early):
                empty_y(t, cols)

        cand_scales = {PLAIN: ca_scales, HASHED: hc_scales}
        cand_words = {}

        def pick_candidates(kind, offsets, part, tag):
            width = part.stop - part.start
            words = keep.tile([P, width], U32, name="words%d_%d" % (kind, part.start), tag=tag, align_bytes=64)
            nc.vector.tensor_copy(words[:], xw[:].bitcast(U32).indirect(entries(offsets, part)))
            for i in range(width // P):
                cand_words[kind, part.start // P + i] = words[:, i * P : (i + 1) * P]

        pick_candidates(HASHED, hc_sb, ALL, "hc_words")

        for t in range(PACK):
            gather("scalar", y_at[t][:, HALVES[0]], y_sb[t][:], n1_sb, HALVES[0])
            gather("vector", y_at[t][:, HALVES[1]], y_sb[t][:], n1_sb, HALVES[1])
            if t == 0:
                nc.gpsimd.tensor_tensor(st[:, t, :], y_sb[t][:], y_at[t][:], ALU.subtract)
            else:
                nc.vector.scalar_tensor_tensor(
                    st[:, t, :], y_ps[t][:], gs_abs[:, t : t + 1], y_at[t][:], ALU.mult, ALU.subtract
                )
            if t + early < PACK:
                empty_y(t + early, ALL)

        z_codes = keep.tile([P, S], U32, name="z_codes", align_bytes=64)
        z_scales = keep.tile([P, S], U8, name="z_scales", align_bytes=64)
        sign_wide = gs_sign[:].unsqueeze(1).to_broadcast([P, QUARTER, PACK])
        b_abs = [keep.tile([P, S], F32, name="b_abs%d" % i) for i in range(TILES)]
        a_sb = [keep.tile([P, S], F32, name="a_sb%d" % i) for i in range(TILES)]
        first_tiles = range(TILES // 2)
        other_tiles = range(TILES // 2, TILES)
        st_at = {}
        z_abs = {}
        acc = {}

        def gather_st(h, tag, on_vector):
            st_at[h] = keep.tile([P, PACK, HALF], F32, name="st_at%d" % h, tag=tag, align_bytes=64)
            for t in range(PACK):
                gather("vector" if t == on_vector else "scalar", st_at[h][:, t, :], st[:, t, :], n2_sb, HALVES[h])

        def quarter(u):
            return slice(u * QUARTER, (u + 1) * QUARTER)

        def largest(u, tag):
            z_abs[u] = keep.tile([P, QUARTER, PACK], BF16, name="z_abs%d" % u, tag=tag, align_bytes=64)
            nc.vector.tensor_tensor(
                z_abs[u][:].rearrange("p (c i) t -> p c t i", i=2),
                st[:, :, quarter(u)].rearrange("p t (c i) -> p c t i", i=2),
                st_at[u // 2][:, :, quarter(u % 2)].rearrange("p t (c i) -> p c t i", i=2),
                ALU.max,
            )

        def quantise_z(h):
            z_bf = {}
            for u in (2 * h, 2 * h + 1):
                z_bf[u] = keep.tile([P, QUARTER, PACK], BF16, name="z_bf%d" % u, tag="z_bf%d" % u, align_bytes=64)
                nc.vector.tensor_tensor(z_bf[u][:], z_abs[u][:], sign_wide, ALU.mult)
            for u in (2 * h, 2 * h + 1):
                nc.vector.quantize_mx(
                    out=z_codes[:, quarter(u)].bitcast(FP8X4),
                    scales=z_scales[:, quarter(u)],
                    in_=z_bf[u][:].rearrange("p n t -> p (n t)"),
                )

        def score(kind, cols, tiles=range(TILES)):
            for i in tiles:
                if (kind, i) not in acc:
                    bank = "bank%d" % (TILES * kind + i)
                    acc[kind, i] = psum.tile([P, S], F32, name="acc%d_%d" % (kind, i), tag=bank)
                rows = slice(i * P, (i + 1) * P)
                mx_product(
                    acc[kind, i][:, cols],
                    cand_words[kind, i],
                    cand_scales[kind][:, rows],
                    z_codes[:, cols],
                    z_scales[:, cols],
                )

        def empty_b(cols):
            for i in range(TILES):
                nc.scalar.activation(b_abs[i][:, cols], acc[HASHED, i][:, cols], ACT.Abs)

        gather_st(0, "st_at0", on_vector=2)
        pick_candidates(PLAIN, ca_sb, HALVES[0], "y_at%d" % (PACK - 2))
        largest(0, "z_abs0")
        largest(1, "z_abs1")
        gather_st(1, "y_at%d" % (PACK - 1), on_vector=None)
        quantise_z(0)
        score(HASHED, HALVES[0])
        score(PLAIN, HALVES[0], first_tiles)
        empty_b(HALVES[0])
        for i in first_tiles:
            nc.scalar.copy(a_sb[i][:, HALVES[0]], acc[PLAIN, i][:, HALVES[0]])
        largest(2, "z_bf0")
        largest(3, "z_bf1")
        quantise_z(1)
        score(HASHED, HALVES[1])
        score(PLAIN, HALVES[1], first_tiles)
        pick_candidates(PLAIN, ca_sb, HALVES[1], "z_bf3")
        score(PLAIN, ALL, other_tiles)
        empty_b(HALVES[1])

        def empty_a(i):
            cols = HALVES[1] if i in first_tiles else ALL
            if i % 2 == 0:
                nc.vector.tensor_copy(a_sb[i][:, cols], acc[PLAIN, i][:, cols])
            else:
                nc.scalar.copy(a_sb[i][:, cols], acc[PLAIN, i][:, cols])

        den = []
        for i in range(TILES):
            b_at = keep.tile([P, S], F32, name="b_at%d" % i)
            for cols in HALVES:
                gather("vector" if i == 0 else "scalar", b_at[:, cols], b_abs[i][:], n4_sb, cols)
            den.append(keep.tile([P, S], F32, name="den%d" % i))
            nc.gpsimd.tensor_tensor(den[i][:], b_abs[i][:], b_at[:], ALU.add)
            if i > 0:
                empty_a(i - 1)

        last = TILES - 1
        for i in range(TILES):
            root = keep.tile([P, S], F32, name="root%d" % i)
            nc.scalar.activation(root[:], den[i][:], ACT.Abs_reciprocal_sqrt, bias=DEN_OFFSET)
            a_at = keep.tile([P, S], F32, name="a_at%d" % i)
            for cols in HALVES:
                gather("vector", a_at[:, cols], a_sb[i][:], n3_sb, cols)
            inv = keep.tile([P, S], F32, name="inv%d" % i)
            nc.scalar.activation(inv[:], root[:], ACT.Square)
            if i + 2 == last:
                empty_a(last)
            parts = HALVES if i == last else (ALL,)
            num = keep.tile([P, S], F32, name="num%d" % i)
            for cols in parts:
                nc.vector.tensor_tensor(num[:, cols], acc[PLAIN, i][:, cols], a_at[:, cols], ALU.subtract)
            finisher = nc.gpsimd if i in first_tiles else nc.vector
            for cols in parts:
                res = keep.tile([P, cols.stop - cols.start], F32, name="res%d_%d" % (i, cols.start))
                finisher.tensor_tensor(res[:], inv[:, cols], num[:, cols], ALU.mult)
                nc.sync.dma_start(out[i * P : (i + 1) * P, cols], res[:])
